import numpy as np
import ml_dtypes


def mxq(x, axis, fmt="e4m3"):
    dtype, down = {"e4m3": (ml_dtypes.float8_e4m3fn, 7), "e5m2": (ml_dtypes.float8_e5m2, 14)}[fmt]
    v = np.moveaxis(np.asarray(x, np.float32).astype(ml_dtypes.bfloat16).astype(np.float64), axis, -1)
    blocks = v.reshape(v.shape[:-1] + (-1, 32))
    amax = np.abs(blocks).max(-1, keepdims=True)
    byte = np.maximum(np.where(amax > 0, np.frexp(amax)[1] - 1 + 127, 0) - down, 1)
    scale = np.exp2(byte - 127.0)
    codes = (blocks / scale).astype(np.float32).astype(dtype).astype(np.float64)
    return np.moveaxis((codes * scale).reshape(v.shape), -1, axis)


WIDE = False


def mx_kscale(k):
    if not WIDE:
        return np.ones(k)
    levels = np.array([10, -10, 5, -5, 0])
    if k % 512:
        return np.exp2(np.random.permutation(np.resize(levels, k // 32))).repeat(32)
    a = np.empty((k // 512, 16))
    for p in range(k // 512):
        a[p, :8] = np.random.permutation(np.resize(levels, 8))
        for g in range(8):
            far = levels[np.abs(levels - a[p, g]) >= 10]
            a[p, g + 8] = far[np.random.randint(len(far))]
    return np.exp2(a.ravel()).repeat(32)


def f64(x):
    return np.asarray(x).astype(np.float64)


def striped(idx):
    return np.tile(idx.reshape(-1, 16).T, (8, 1)).astype(np.uint16)


def unstriped(offs):
    return offs[:16].T.reshape(-1).astype(np.int64)


E2M1 = np.array([0.0, 0.5, 1.0, 1.5, 2.0, 3.0, 4.0, 6.0, -0.0, -0.5, -1.0, -1.5, -2.0, -3.0, -4.0, -6.0])


def pack_weight(w, fmt):
    k, n = w.shape
    w = f64(np.asarray(w, np.float32).astype(ml_dtypes.bfloat16)).reshape(k // 32, 32, n)
    amax = np.abs(w).max(1)
    if fmt == "e4m3":
        byte = np.frexp(amax)[1] - 1 + 127 - 7
    else:
        mant, ex = np.frexp(amax / 6.0)
        byte = np.where(mant > 0.5, ex, ex - 1) + 127
    byte = np.clip(np.where(amax > 0, byte, 1), 1, 254)
    scaled = (w * np.exp2(127.0 - byte)[:, None, :]).reshape(k, n).astype(np.float32)
    by_word = np.ascontiguousarray(scaled.reshape(k // 512, 128, 4, n).transpose(0, 1, 3, 2))
    if fmt == "e4m3":
        words = by_word.astype(ml_dtypes.float8_e4m3fn).view(np.uint8)
    else:
        c = by_word.astype(ml_dtypes.float4_e2m1fn).view(np.uint8) & 0xF
        words = (c[..., 0::2] | (c[..., 1::2] << 4)).reshape(k // 512, 128, 2 * n)
    return np.ascontiguousarray(words), np.ascontiguousarray(byte.astype(np.uint8).reshape(k // 512, 16, n))


def unpack_weight(words, scales, fmt):
    g, _, n = scales.shape
    words = np.ascontiguousarray(words).reshape(g, 128, n, -1)
    if fmt == "e4m3":
        vals = words.view(ml_dtypes.float8_e4m3fn).astype(np.float64)
    else:
        nib = np.empty((g, 128, n, 4), np.uint8)
        nib[..., 0::2] = words & 0xF
        nib[..., 1::2] = words >> 4
        vals = E2M1[nib]
    vals = vals * np.repeat(np.exp2(scales.astype(np.float64) - 127.0), 8, axis=1)[..., None]
    return vals.transpose(0, 1, 3, 2).reshape(g * 512, n)


def gelu(v):
    return 0.5 * v * (1.0 + np.tanh(np.sqrt(2.0 / np.pi) * (v + 0.044715 * v**3)))


def striped8(idx):
    return np.concatenate([v.reshape(-1, 16).T for v in idx]).astype(np.uint16)


def unstriped8(offs):
    return np.stack([offs[16 * g:16 * g + 16].T.reshape(-1) for g in range(8)]).astype(np.int64)


def heads(h, wgt, idx8):
    r = np.arange(h.shape[0])
    return wgt[r // 4 % 128] * h[r[:, None], idx8[r % 512 // 64]]


def put_heads(h, wgs, idx8, t2):
    r = np.arange(h.shape[0])
    page = np.zeros((h.shape[0], t2))
    page[r[:, None], idx8[r % 512 // 64]] = wgs[r // 4 % 128] * h
    return page


K, H, N, T, S, P, T2 = 1024, 1024, 512, 2048, 1024, 512, 1024

def setup_inputs():
    n = np.random.standard_normal
    s = mx_kscale(K)[:, None]
    u = mx_kscale(H)[:, None]
    d = {}
    d["tab_words"], d["tab_scales"] = pack_weight(n((K, T)) * s, "e4m3")
    d["offs"] = striped(np.random.permutation(T)[:S])
    d["offs2"] = striped8(np.stack([np.random.permutation(S)[:P] for _ in range(8)]))
    d["offs3"] = striped8(np.stack([np.random.permutation(T2)[:P] for _ in range(8)]))
    d["w1"] = (n((K, H)) / s * u.T / K**0.5).astype(np.float32)
    d["b1"] = (0.5 * n(H) * u[:, 0]).astype(np.float32)
    d["level"] = (0.6 * n(H) * u[:, 0]).astype(np.float32)
    d["wgt"] = np.repeat(np.random.uniform(0.5, 2.0, (8, P)), 16, axis=0).astype(np.float32)
    d["w2"] = (n((H, N)) / u / H**0.5).astype(np.float32)
    d["w3_words"], d["w3_scales"] = pack_weight(n((H, N)) / u / H**0.5, "e2m1")
    d["wgo"] = np.repeat(np.random.uniform(0.5, 2.0, (8, P)), 16, axis=0).astype(np.float32)
    return d

def reference(tab_words, tab_scales, offs, offs2, offs3, w1, b1, level, wgt, w2, w3_words, w3_scales, wgo):
    v = unpack_weight(tab_words, tab_scales, "e4m3")[:, unstriped(offs)]
    h = (mxq(f64(w1), 0, "e4m3").T @ v) + f64(b1)[:, None]
    x = heads(h, f64(wgt), unstriped8(offs2))
    hi = np.maximum(x, f64(level)[:, None])
    lo = np.minimum(x, f64(level)[:, None])
    y1 = mxq(f64(w2), 0, "e4m3").T @ mxq(hi, 0, "e4m3")
    y2 = unpack_weight(w3_words, w3_scales, "e2m1").T @ mxq(lo, 0, "e4m3")
    y = y1 * y2 + y1
    return put_heads(y, f64(wgo), unstriped8(offs3), T2)

@@ -1,0 +1,275 @@
+from contextlib import ExitStack
+
+import concourse.mybir as mybir
+
+K, H, N, T, S, M, T2 = 1024, 1024, 512, 2048, 1024, 512, 1024
+FLOPS = 2 * K * H * S + 2 * 2 * H * N * M
+
+F32 = mybir.dt.float32
+BF16 = mybir.dt.bfloat16
+I32 = mybir.dt.int32
+U32 = mybir.dt.uint32
+U16 = mybir.dt.uint16
+U8 = mybir.dt.uint8
+FP8X4 = mybir.dt.float8_e4m3fn_x4
+FP4X4 = mybir.dt.float4_e2m1fn_x4
+ALU = mybir.AluOpType
+ACT = mybir.ActivationFunctionType
+
+P = 128
+PACK = 4
+PASS = P * PACK
+BANK = 512
+
+
+def tile_list_fluency_cue_feedback_kernel(
+    tc, tab_words, tab_scales, offs, offs2, offs3, w1, b1, level, wgt, w2, w3_words, w3_scales, wgo, out
+):
+    nc = tc.nc
+    with ExitStack() as ctx:
+        sb = ctx.enter_context(tc.tile_pool(name="sb", bufs=1))
+        psum = ctx.enter_context(tc.psum_pool(name="psum", bufs=8))
+
+        def tile(shape, dtype, name, tag=None):
+            return sb.tile(shape, dtype, name=name, tag=tag or name, align_bytes=64)
+
+        def bank():
+            return psum.tile([P, BANK], F32, name="bank")
+
+        def load_rows(w, a, cols, name):
+            raw = tile([P, PACK, cols.stop - cols.start], F32, name)
+            nc.sync.dma_start(out=raw[:], in_=w[PASS * a : PASS * (a + 1), cols].rearrange("(p j) c -> p j c", j=PACK))
+            return raw
+
+        def deal(copy, grouped, raw, pair, q0):
+            width = raw.shape[2] // PACK
+            copy(
+                out=grouped[:, :, q0 : q0 + width, :].rearrange("p t q j -> p q j t"),
+                in_=raw[:].rearrange("p j (q t) -> p q j t", t=PACK)[:, :, :, 2 * pair : 2 * pair + 2],
+            )
+
+        def quantize(grouped, name):
+            width = grouped.shape[1] // PACK
+            codes = tile([P, width], U32, name + "_codes")
+            scales = tile([P, width], U8, name + "_scales")
+            nc.vector.quantize_mx(out=codes[:].bitcast(FP8X4), scales=scales[:], in_=grouped)
+            return codes, scales
+
+        def flat(grouped):
+            return grouped[:].rearrange("p t q j -> p (t q j)")
+
+        tab_s = tile([P, T], U8, "tab_s")
+        nc.vector.memset(tab_s[:].bitcast(I32), 0)
+        w3_s_raw = tile([P, 2, N], U8, "w3_s_raw")
+        nc.vector.memset(w3_s_raw[:].bitcast(I32), 0)
+        pages = [tile([P, T2], F32, f"page{t}") for t in range(PACK)]
+        for t in range(PACK):
+            nc.vector.memset(pages[t][:], 0.0)
+
+        list1 = sb.tile([P, S // 16], U16, name="list1")
+        list2 = sb.tile([P, M // 16], U16, name="list2")
+        list3 = sb.tile([P, M // 16], U16, name="list3")
+        tab_w = [tile([P, T], I32, f"tab_w{a}") for a in range(2)]
+
+        def load_table(a):
+            nc.sync.dma_start(out=tab_w[a][:], in_=tab_words[a].rearrange("p t i -> p (t i)").bitcast(I32))
+
+        bias = tile([P, 2, PACK], F32, "bias")
+        lev = tile([P, 2, PACK], F32, "lev")
+        nc.sync.dma_start(list1[:], offs)
+        nc.sync.dma_start(out=lev[:], in_=level.rearrange("(b p t) -> p b t", b=2, t=PACK))
+        load_table(0)
+        for q in range(4):
+            nc.sync.dma_start(
+                out=tab_s[32 * q : 32 * q + 8, :].bitcast(I32),
+                in_=tab_scales[:, 4 * q : 4 * q + 4, :].bitcast(I32),
+            )
+        w1_raw = {}
+        w1_raw[0, 0] = [load_rows(w1, 0, slice(0, PASS), "w1_raw00")]
+        load_table(1)
+        w1_raw[1, 0] = [load_rows(w1, 1, slice(256 * u, 256 * (u + 1)), f"w1_raw10_{u}") for u in range(2)]
+        nc.sync.dma_start(out=bias[:], in_=b1.rearrange("(b p t) -> p b t", b=2, t=PACK))
+        nc.sync.dma_start(list2[:], offs2)
+        wgt_sb = tile([P, M], F32, "wgt_sb")
+        nc.sync.dma_start(out=wgt_sb[:], in_=wgt)
+        for a in range(2):
+            w1_raw[a, 1] = [load_rows(w1, a, slice(PASS, 2 * PASS), f"w1_raw{a}1")]
+        w3_w_raw = tile([P, 2, 2 * N], U8, "w3_w_raw")
+        nc.sync.dma_start(out=w3_w_raw[:].bitcast(I32), in_=w3_words.rearrange("a p c -> p a c").bitcast(I32))
+        for q in range(4):
+            nc.sync.dma_start(
+                out=w3_s_raw[32 * q : 32 * q + 4, :, :].bitcast(I32),
+                in_=w3_scales[:, 4 * q : 4 * q + 4, :].rearrange("a r c -> r a c").bitcast(I32),
+            )
+        w2_raw = [load_rows(w2, b, slice(0, N), f"w2_raw{b}") for b in range(2)]
+        nc.sync.dma_start(list3[:], offs3)
+        wgo_sb = tile([P, M], F32, "wgo_sb")
+        nc.sync.dma_start(out=wgo_sb[:], in_=wgo)
+
+        lev_bf = tile([P, 2, PACK], BF16, "lev_bf")
+        nc.scalar.activation(out=lev_bf[:], in_=lev[:], func=ACT.Identity)
+
+        v_w = [tile([P, S], U32, f"v_w{a}") for a in range(2)]
+        v_s = tile([P, S], U8, "v_s")
+        nc.vector.tensor_copy(v_w[0][:], tab_w[0][:].bitcast(U32).indirect(list1[:]))
+        nc.vector.tensor_copy(v_s[:], tab_s[:].indirect(list1[:]))
+
+        w1_g = {(a, b, pr): tile([P, 2, P, PACK], BF16, f"w1_g{a}{b}{pr}") for a in range(2) for b in range(2) for pr in range(2)}
+        w1_q = {}
+        for pr in range(2):
+            deal(nc.scalar.copy, w1_g[0, 0, pr], w1_raw[0, 0][0], pr, 0)
+        for hf in range(2):
+            nc.vector.tensor_copy(
+                v_w[1][:, BANK * hf : BANK * (hf + 1)],
+                tab_w[1][:].bitcast(U32).indirect(list1[:, 32 * hf : 32 * (hf + 1)]),
+            )
+            w1_q[0, 0, hf] = quantize(flat(w1_g[0, 0, hf]), f"w1_q00{hf}")
+        deal(nc.scalar.copy, w1_g[1, 0, 0], w1_raw[1, 0][0], 0, 0)
+        deal(nc.vector.tensor_copy, w1_g[1, 0, 0], w1_raw[1, 0][1], 0, 64)
+        deal(nc.scalar.copy, w1_g[1, 0, 1], w1_raw[1, 0][0], 1, 0)
+        deal(nc.scalar.copy, w1_g[1, 0, 1], w1_raw[1, 0][1], 1, 64)
+        for pr in range(2):
+            w1_q[1, 0, pr] = quantize(flat(w1_g[1, 0, pr]), f"w1_q10{pr}")
+
+        def stage1_pass(acc, a, b, t, hf):
+            codes, scales = w1_q[a, b, t // 2]
+            wc = slice(P * (t % 2), P * (t % 2 + 1))
+            sc = slice(BANK * hf, BANK * (hf + 1))
+            nc.tensor.matmul_mx(
+                out=acc[:],
+                lhsT=codes[:, wc].bitcast(FP8X4),
+                lhsT_scale=scales[:, wc],
+                rhs=v_w[a][:, sc].bitcast(FP8X4),
+                rhs_scale=v_s[4 * a : P, sc],
+                start=(a == 0),
+                stop=(a == 1),
+            )
+
+        h = {(b, t): tile([P, S], F32, f"h{b}{t}") for b in range(2) for t in range(PACK)}
+        x = [tile([P, PACK, M], F32, f"x{b}") for b in range(2)]
+
+        def evacuate(acc, b, t, hf):
+            nc.scalar.activation(
+                out=h[b, t][:, BANK * hf : BANK * (hf + 1)], in_=acc[:], func=ACT.Identity, bias=bias[:, b, t : t + 1]
+            )
+
+        def pick(b, t):
+            nc.vector.tensor_tensor(x[b][:, t, :], h[b, t][:].indirect(list2[:]), wgt_sb[:], ALU.mult)
+
+        accs = {(t, hf): bank() for t in range(PACK) for hf in range(2)}
+        for a in range(2):
+            for t in range(PACK):
+                for hf in range(2):
+                    stage1_pass(accs[t, hf], a, 0, t, hf)
+
+        w3_w = tile([P, 2, PACK, P, 2], U8, "w3_w")
+        w3_s = tile([P, 2, PACK, P], U8, "w3_s")
+        nc.vector.tensor_copy(
+            out=w3_w[:].rearrange("p a t q e -> p a q t e"),
+            in_=w3_w_raw[:].rearrange("p a (q t e) -> p a q t e", t=PACK, e=2),
+        )
+        nc.vector.tensor_copy(
+            out=w3_s[:].rearrange("p a t q -> p a q t"),
+            in_=w3_s_raw[:].rearrange("p a (q t) -> p a q t", t=PACK),
+        )
+
+        for t in range(PACK):
+            for hf in range(2):
+                evacuate(accs[t, hf], 0, t, hf)
+            pick(0, t)
+            if t % 2 == 1:
+                pr = t // 2
+                for a in range(2):
+                    deal(nc.scalar.copy, w1_g[a, 1, pr], w1_raw[a, 1][0], pr, 0)
+                    w1_q[a, 1, pr] = quantize(flat(w1_g[a, 1, pr]), f"w1_q{a}1{pr}")
+
+        for t in range(PACK):
+            for hf in range(2):
+                acc = bank()
+                for a in range(2):
+                    stage1_pass(acc, a, 1, t, hf)
+                evacuate(acc, 1, t, hf)
+            pick(1, t)
+
+        x_bf = [tile([P, M, PACK], BF16, f"x_bf{b}") for b in range(2)]
+        hi = [tile([P, M, PACK], BF16, f"hi{b}") for b in range(2)]
+        lo = [tile([P, M, PACK], BF16, f"lo{b}") for b in range(2)]
+        w2_g = {(b, pr): tile([P, 2, P, PACK], BF16, f"w2_g{b}{pr}") for b in range(2) for pr in range(2)}
+        w2_q, hi_q, lo_q = {}, {}, {}
+
+        def weave(b):
+            for u in range(2):
+                cols = slice(256 * u, 256 * (u + 1))
+                nc.scalar.copy(
+                    out=x_bf[b][:, cols, :].rearrange("p (c i) t -> p c t i", i=4),
+                    in_=x[b][:, :, cols].rearrange("p t (c i) -> p c t i", i=4),
+                )
+
+        def split(b):
+            lv = lev_bf[:, b : b + 1, :].to_broadcast([P, M, PACK])
+            nc.vector.tensor_tensor(lo[b][:], x_bf[b][:], lv, ALU.min)
+            nc.vector.tensor_tensor(hi[b][:], x_bf[b][:], lv, ALU.max)
+            lo_q[b] = quantize(lo[b][:].rearrange("p m t -> p (m t)"), f"lo_q{b}")
+            hi_q[b] = quantize(hi[b][:].rearrange("p m t -> p (m t)"), f"hi_q{b}")
+
+        def deal_w2(pr):
+            for b in range(2):
+                deal(nc.scalar.copy, w2_g[b, pr], w2_raw[b], pr, 0)
+                w2_q[b, pr] = quantize(flat(w2_g[b, pr]), f"w2_q{b}{pr}")
+
+        weave(0)
+        weave(1)
+        split(0)
+        deal_w2(0)
+        split(1)
+        deal_w2(1)
+
+        y1 = [bank() for t in range(PACK)]
+        y2 = [bank() for t in range(PACK)]
+
+        def y2_pass(b, t):
+            codes, scales = lo_q[b]
+            nc.tensor.matmul_mx(
+                out=y2[t][:],
+                lhsT=w3_w[:, b, t, :, :].rearrange("p q e -> p (q e)").bitcast(FP4X4),
+                lhsT_scale=w3_s[:, b, t, :],
+                rhs=codes[:].bitcast(FP8X4),
+                rhs_scale=scales[:],
+                start=(b == 0),
+                stop=(b == 1),
+            )
+
+        def y1_pass(b, t):
+            codes, scales = hi_q[b]
+            w_codes, w_scales = w2_q[b, t // 2]
+            wc = slice(P * (t % 2), P * (t % 2 + 1))
+            nc.tensor.matmul_mx(
+                out=y1[t][:],
+                lhsT=w_codes[:, wc].bitcast(FP8X4),
+                lhsT_scale=w_scales[:, wc],
+                rhs=codes[:].bitcast(FP8X4),
+                rhs_scale=scales[:],
+                start=(b == 0),
+                stop=(b == 1),
+            )
+
+        for b in range(2):
+            for t in range(PACK):
+                y2_pass(b, t)
+            for t in range(PACK):
+                y1_pass(b, t)
+
+        out_rows = out.rearrange("(p t) c -> p t c", t=PACK)
+        first = [tile([P, M], F32, f"first{t}", tag=f"w1_g0{t // 2}{t % 2}") for t in range(PACK)]
+        second = [tile([P, M], F32, f"second{t}", tag=f"w1_g1{t // 2}{t % 2}") for t in range(PACK)]
+
+        def factors(t):
+            nc.vector.scalar_tensor_tensor(second[t][:], y2[t][:], 1.0, wgo_sb[:], ALU.add, ALU.mult)
+            nc.scalar.copy(out=first[t][:], in_=y1[t][:])
+
+        factors(0)
+        for t in range(PACK):
+            if t + 1 < PACK:
+                factors(t + 1)
+            nc.vector.tensor_tensor(pages[t][:].indirect(list3[:]), first[t][:], second[t][:], ALU.mult)
+            nc.sync.dma_start(out=out_rows[:, t, :], in_=pages[t][:])

@@ -74,11 +74,11 @@ def tile_list_fluency_cue_feedback_kernel(
         def load_table(a):
             nc.sync.dma_start(out=tab_w[a][:], in_=tab_words[a].rearrange("p t i -> p (t i)").bitcast(I32))
 
-        bias = tile([P, 2, PACK], F32, "bias")
-        lev = tile([P, 2, PACK], F32, "lev")
+        bias = tile([P, 2, 2 * PACK], F32, "bias")
+        lev = tile([P, 2, 2 * PACK], F32, "lev")
         nc.sync.dma_start(list1[:], offs)
-        nc.sync.dma_start(out=lev[:], in_=level.rearrange("(b p t) -> p b t", b=2, t=PACK))
         load_table(0)
+        nc.sync.dma_start(out=lev[:, :, 0:PACK], in_=level.rearrange("(b p t) -> p b t", b=2, t=PACK))
         for q in range(4):
             nc.sync.dma_start(
                 out=tab_s[32 * q : 32 * q + 8, :].bitcast(I32),
@@ -88,8 +88,8 @@ def tile_list_fluency_cue_feedback_kernel(
         w1_raw[0, 0] = [load_rows(w1, 0, slice(0, PASS), "w1_raw00")]
         load_table(1)
         w1_raw[1, 0] = [load_rows(w1, 1, slice(256 * u, 256 * (u + 1)), f"w1_raw10_{u}") for u in range(2)]
-        nc.sync.dma_start(out=bias[:], in_=b1.rearrange("(b p t) -> p b t", b=2, t=PACK))
         nc.sync.dma_start(list2[:], offs2)
+        nc.sync.dma_start(out=bias[:, :, 0:PACK], in_=b1.rearrange("(b p t) -> p b t", b=2, t=PACK))
         wgt_sb = tile([P, M], F32, "wgt_sb")
         nc.sync.dma_start(out=wgt_sb[:], in_=wgt)
         for a in range(2):
@@ -106,15 +106,12 @@ def tile_list_fluency_cue_feedback_kernel(
         wgo_sb = tile([P, M], F32, "wgo_sb")
         nc.sync.dma_start(out=wgo_sb[:], in_=wgo)
 
-        lev_bf = tile([P, 2, PACK], BF16, "lev_bf")
-        nc.scalar.activation(out=lev_bf[:], in_=lev[:], func=ACT.Identity)
-
         v_w = [tile([P, S], U32, f"v_w{a}") for a in range(2)]
         v_s = tile([P, S], U8, "v_s")
         nc.vector.tensor_copy(v_w[0][:], tab_w[0][:].bitcast(U32).indirect(list1[:]))
         nc.vector.tensor_copy(v_s[:], tab_s[:].indirect(list1[:]))
 
-        w1_g = {(a, b, pr): tile([P, 2, P, PACK], BF16, f"w1_g{a}{b}{pr}") for a in range(2) for b in range(2) for pr in range(2)}
+        w1_g = {(a, 0, pr): tile([P, 2, P, PACK], BF16, f"w1_g{a}0{pr}") for a in range(2) for pr in range(2)}
         w1_q = {}
         for pr in range(2):
             deal(nc.scalar.copy, w1_g[0, 0, pr], w1_raw[0, 0][0], pr, 0)
@@ -124,10 +121,9 @@ def tile_list_fluency_cue_feedback_kernel(
                 tab_w[1][:].bitcast(U32).indirect(list1[:, 32 * hf : 32 * (hf + 1)]),
             )
             w1_q[0, 0, hf] = quantize(flat(w1_g[0, 0, hf]), f"w1_q00{hf}")
-        deal(nc.scalar.copy, w1_g[1, 0, 0], w1_raw[1, 0][0], 0, 0)
-        deal(nc.vector.tensor_copy, w1_g[1, 0, 0], w1_raw[1, 0][1], 0, 64)
-        deal(nc.scalar.copy, w1_g[1, 0, 1], w1_raw[1, 0][0], 1, 0)
-        deal(nc.scalar.copy, w1_g[1, 0, 1], w1_raw[1, 0][1], 1, 64)
+        for u in range(2):
+            for pr in range(2):
+                deal(nc.scalar.copy, w1_g[1, 0, pr], w1_raw[1, 0][u], pr, 64 * u)
         for pr in range(2):
             w1_q[1, 0, pr] = quantize(flat(w1_g[1, 0, pr]), f"w1_q10{pr}")
 
@@ -162,28 +158,15 @@ def tile_list_fluency_cue_feedback_kernel(
                 for hf in range(2):
                     stage1_pass(accs[t, hf], a, 0, t, hf)
 
-        w3_w = tile([P, 2, PACK, P, 2], U8, "w3_w")
-        w3_s = tile([P, 2, PACK, P], U8, "w3_s")
-        nc.vector.tensor_copy(
-            out=w3_w[:].rearrange("p a t q e -> p a q t e"),
-            in_=w3_w_raw[:].rearrange("p a (q t e) -> p a q t e", t=PACK, e=2),
-        )
-        nc.vector.tensor_copy(
-            out=w3_s[:].rearrange("p a t q -> p a q t"),
-            in_=w3_s_raw[:].rearrange("p a (q t) -> p a q t", t=PACK),
-        )
-
-        for t in range(PACK):
+        def first_block(t):
             for hf in range(2):
-                evacuate(accs[t, hf], 0, t, hf)
+                if (t, hf) == (0, 1):
+                    nc.vector.tensor_scalar(h[0, 0][:, BANK:], accs[t, hf][:], bias[:, 0, 0:1], None, ALU.add)
+                else:
+                    evacuate(accs[t, hf], 0, t, hf)
             pick(0, t)
-            if t % 2 == 1:
-                pr = t // 2
-                for a in range(2):
-                    deal(nc.scalar.copy, w1_g[a, 1, pr], w1_raw[a, 1][0], pr, 0)
-                    w1_q[a, 1, pr] = quantize(flat(w1_g[a, 1, pr]), f"w1_q{a}1{pr}")
 
-        for t in range(PACK):
+        def second_block(t):
             for hf in range(2):
                 acc = bank()
                 for a in range(2):
@@ -191,37 +174,81 @@ def tile_list_fluency_cue_feedback_kernel(
                 evacuate(acc, 1, t, hf)
             pick(1, t)
 
+        def deal_w1(a, pr):
+            w1_g[a, 1, pr] = tile([P, 2, P, PACK], BF16, f"w1_g{a}1{pr}", tag=f"w1_q10{pr}_" + ("codes", "scales")[a])
+            deal(nc.scalar.copy, w1_g[a, 1, pr], w1_raw[a, 1][0], pr, 0)
+            w1_q[a, 1, pr] = quantize(flat(w1_g[a, 1, pr]), f"w1_q{a}1{pr}")
+
+        lev_bf = tile([P, 2, 16, PACK], BF16, "lev_bf")
         x_bf = [tile([P, M, PACK], BF16, f"x_bf{b}") for b in range(2)]
         hi = [tile([P, M, PACK], BF16, f"hi{b}") for b in range(2)]
         lo = [tile([P, M, PACK], BF16, f"lo{b}") for b in range(2)]
-        w2_g = {(b, pr): tile([P, 2, P, PACK], BF16, f"w2_g{b}{pr}") for b in range(2) for pr in range(2)}
+        w2_g = {}
         w2_q, hi_q, lo_q = {}, {}, {}
 
-        def weave(b):
-            for u in range(2):
-                cols = slice(256 * u, 256 * (u + 1))
-                nc.scalar.copy(
-                    out=x_bf[b][:, cols, :].rearrange("p (c i) t -> p c t i", i=4),
-                    in_=x[b][:, :, cols].rearrange("p t (c i) -> p c t i", i=4),
-                )
+        def weave(b, u):
+            cols = slice(256 * u, 256 * (u + 1))
+            nc.scalar.copy(
+                out=x_bf[b][:, cols, :].rearrange("p (c i) t -> p c t i", i=4),
+                in_=x[b][:, :, cols].rearrange("p t (c i) -> p c t i", i=4),
+            )
 
-        def split(b):
-            lv = lev_bf[:, b : b + 1, :].to_broadcast([P, M, PACK])
-            nc.vector.tensor_tensor(lo[b][:], x_bf[b][:], lv, ALU.min)
-            nc.vector.tensor_tensor(hi[b][:], x_bf[b][:], lv, ALU.max)
-            lo_q[b] = quantize(lo[b][:].rearrange("p m t -> p (m t)"), f"lo_q{b}")
-            hi_q[b] = quantize(hi[b][:].rearrange("p m t -> p (m t)"), f"hi_q{b}")
+        for b in range(2):
+            lo_q[b] = (tile([P, M], U32, f"lo_codes{b}"), tile([P, M], U8, f"lo_scales{b}"))
+            hi_q[b] = (tile([P, M], U32, f"hi_codes{b}"), tile([P, M], U8, f"hi_scales{b}"))
+
+        def split(b, u):
+            cols = slice(256 * u, 256 * (u + 1))
+            lv = lev_bf[:, b : b + 1, :, :].rearrange("p b m t -> p b (m t)").to_broadcast([P, 16, 16 * PACK])
+            for part, op in ((lo[b], ALU.min), (hi[b], ALU.max)):
+                nc.vector.tensor_tensor(
+                    part[:, cols, :].rearrange("p (c m) t -> p c (m t)", m=16),
+                    x_bf[b][:, cols, :].rearrange("p (c m) t -> p c (m t)", m=16),
+                    lv,
+                    op,
+                )
+            for part, (codes, scales) in ((lo[b], lo_q[b]), (hi[b], hi_q[b])):
+                nc.vector.quantize_mx(
+                    out=codes[:, cols].bitcast(FP8X4),
+                    scales=scales[:, cols],
+                    in_=part[:, cols, :].rearrange("p m t -> p (m t)"),
+                )
 
         def deal_w2(pr):
             for b in range(2):
+                tag = ("w1_q111_" + ("codes", "scales")[b], f"x{b}")[pr]
+                w2_g[b, pr] = tile([P, 2, P, PACK], BF16, f"w2_g{b}{pr}", tag=tag)
                 deal(nc.scalar.copy, w2_g[b, pr], w2_raw[b], pr, 0)
                 w2_q[b, pr] = quantize(flat(w2_g[b, pr]), f"w2_q{b}{pr}")
 
-        weave(0)
-        weave(1)
-        split(0)
+        first_block(0)
+        first_block(1)
+        deal_w1(0, 0)
+        first_block(2)
+        deal_w1(1, 0)
+        w3_w = tile([P, 2, PACK, P, 2], U8, "w3_w", tag="w1_q100_scales")
+        nc.vector.tensor_copy(
+            out=w3_w[:].rearrange("p a t q e -> p a t (q e)").bitcast(U16),
+            in_=w3_w_raw[:].bitcast(U16).rearrange("p a (q t) -> p a t q", t=PACK),
+        )
+        first_block(3)
+        second_block(0)
+        deal_w1(0, 1)
+        w3_s = tile([P, 2, PACK, P], U8, "w3_s", tag="w1_q101_codes")
+        nc.vector.tensor_copy(out=w3_s[:], in_=w3_s_raw[:].rearrange("p a (q t) -> p a t q", t=PACK))
+        second_block(1)
+        deal_w1(1, 1)
+        nc.scalar.copy(out=lev_bf[:], in_=lev[:, :, 0:PACK].unsqueeze(2).to_broadcast([P, 2, 16, PACK]))
+        weave(0, 0)
+        split(0, 0)
+        second_block(2)
+        second_block(3)
+        weave(0, 1)
+        split(0, 1)
+        for u in range(2):
+            weave(1, u)
+            split(1, u)
         deal_w2(0)
-        split(1)
         deal_w2(1)
 
         y1 = [bank() for t in range(PACK)]
@@ -260,8 +287,8 @@ def tile_list_fluency_cue_feedback_kernel(
                 y1_pass(b, t)
 
         out_rows = out.rearrange("(p t) c -> p t c", t=PACK)
-        first = [tile([P, M], F32, f"first{t}", tag=f"w1_g0{t // 2}{t % 2}") for t in range(PACK)]
-        second = [tile([P, M], F32, f"second{t}", tag=f"w1_g1{t // 2}{t % 2}") for t in range(PACK)]
+        first = [tile([P, M], F32, f"first{t}", tag=f"w1_g{t // 2}0{t % 2}") for t in range(PACK)]
+        second = [tile([P, M], F32, f"second{t}") for t in range(PACK)]
 
         def factors(t):
             nc.vector.scalar_tensor_tensor(second[t][:], y2[t][:], 1.0, wgo_sb[:], ALU.add, ALU.mult)

from contextlib import ExitStack

import concourse.mybir as mybir

K, H, N, T, S, M, T2 = 1024, 1024, 512, 2048, 1024, 512, 1024
FLOPS = 2 * K * H * S + 2 * 2 * H * N * M

F32 = mybir.dt.float32
BF16 = mybir.dt.bfloat16
I32 = mybir.dt.int32
U32 = mybir.dt.uint32
U16 = mybir.dt.uint16
U8 = mybir.dt.uint8
FP8X4 = mybir.dt.float8_e4m3fn_x4
FP4X4 = mybir.dt.float4_e2m1fn_x4
ALU = mybir.AluOpType
ACT = mybir.ActivationFunctionType

P = 128
PACK = 4
PASS = P * PACK
BANK = 512


def tile_list_fluency_cue_feedback_kernel(
    tc, tab_words, tab_scales, offs, offs2, offs3, w1, b1, level, wgt, w2, w3_words, w3_scales, wgo, out
):
    nc = tc.nc
    with ExitStack() as ctx:
        sb = ctx.enter_context(tc.tile_pool(name="sb", bufs=1))
        psum = ctx.enter_context(tc.psum_pool(name="psum", bufs=8))

        def tile(shape, dtype, name, tag=None):
            return sb.tile(shape, dtype, name=name, tag=tag or name, align_bytes=64)

        def bank():
            return psum.tile([P, BANK], F32, name="bank")

        def load_rows(w, a, cols, name):
            raw = tile([P, PACK, cols.stop - cols.start], F32, name)
            nc.sync.dma_start(out=raw[:], in_=w[PASS * a : PASS * (a + 1), cols].rearrange("(p j) c -> p j c", j=PACK))
            return raw

        def deal(copy, grouped, raw, pair, q0):
            width = raw.shape[2] // PACK
            copy(
                out=grouped[:, :, q0 : q0 + width, :].rearrange("p t q j -> p q j t"),
                in_=raw[:].rearrange("p j (q t) -> p q j t", t=PACK)[:, :, :, 2 * pair : 2 * pair + 2],
            )

        def quantize(grouped, name):
            width = grouped.shape[1] // PACK
            codes = tile([P, width], U32, name + "_codes")
            scales = tile([P, width], U8, name + "_scales")
            nc.vector.quantize_mx(out=codes[:].bitcast(FP8X4), scales=scales[:], in_=grouped)
            return codes, scales

        def flat(grouped):
            return grouped[:].rearrange("p t q j -> p (t q j)")

        tab_s = tile([P, T], U8, "tab_s")
        nc.vector.memset(tab_s[:].bitcast(I32), 0)
        w3_s_raw = tile([P, 2, N], U8, "w3_s_raw")
        nc.vector.memset(w3_s_raw[:].bitcast(I32), 0)
        pages = [tile([P, T2], F32, f"page{t}") for t in range(PACK)]
        for t in range(PACK):
            nc.vector.memset(pages[t][:], 0.0)

        list1 = sb.tile([P, S // 16], U16, name="list1")
        list2 = sb.tile([P, M // 16], U16, name="list2")
        list3 = sb.tile([P, M // 16], U16, name="list3")
        tab_w = [tile([P, T], I32, f"tab_w{a}") for a in range(2)]

        def load_table(a):
            nc.sync.dma_start(out=tab_w[a][:], in_=tab_words[a].rearrange("p t i -> p (t i)").bitcast(I32))

        bias = tile([P, 2, 2 * PACK], F32, "bias")
        lev = tile([P, 2, 2 * PACK], F32, "lev")
        nc.sync.dma_start(list1[:], offs)
        load_table(0)
        nc.sync.dma_start(out=lev[:, :, 0:PACK], in_=level.rearrange("(b p t) -> p b t", b=2, t=PACK))
        for q in range(4):
            nc.sync.dma_start(
                out=tab_s[32 * q : 32 * q + 8, :].bitcast(I32),
                in_=tab_scales[:, 4 * q : 4 * q + 4, :].bitcast(I32),
            )
        w1_raw = {}
        w1_raw[0, 0] = [load_rows(w1, 0, slice(0, PASS), "w1_raw00")]
        load_table(1)
        w1_raw[1, 0] = [load_rows(w1, 1, slice(256 * u, 256 * (u + 1)), f"w1_raw10_{u}") for u in range(2)]
        nc.sync.dma_start(list2[:], offs2)
        nc.sync.dma_start(out=bias[:, :, 0:PACK], in_=b1.rearrange("(b p t) -> p b t", b=2, t=PACK))
        wgt_sb = tile([P, M], F32, "wgt_sb")
        nc.sync.dma_start(out=wgt_sb[:], in_=wgt)
        for a in range(2):
            w1_raw[a, 1] = [load_rows(w1, a, slice(PASS, 2 * PASS), f"w1_raw{a}1")]
        w3_w_raw = tile([P, 2, 2 * N], U8, "w3_w_raw")
        nc.sync.dma_start(out=w3_w_raw[:].bitcast(I32), in_=w3_words.rearrange("a p c -> p a c").bitcast(I32))
        for q in range(4):
            nc.sync.dma_start(
                out=w3_s_raw[32 * q : 32 * q + 4, :, :].bitcast(I32),
                in_=w3_scales[:, 4 * q : 4 * q + 4, :].rearrange("a r c -> r a c").bitcast(I32),
            )
        w2_raw = [load_rows(w2, b, slice(0, N), f"w2_raw{b}") for b in range(2)]
        nc.sync.dma_start(list3[:], offs3)
        wgo_sb = tile([P, M], F32, "wgo_sb")
        nc.sync.dma_start(out=wgo_sb[:], in_=wgo)

        v_w = [tile([P, S], U32, f"v_w{a}") for a in range(2)]
        v_s = tile([P, S], U8, "v_s")
        nc.vector.tensor_copy(v_w[0][:], tab_w[0][:].bitcast(U32).indirect(list1[:]))
        nc.vector.tensor_copy(v_s[:], tab_s[:].indirect(list1[:]))

        w1_g = {(a, 0, pr): tile([P, 2, P, PACK], BF16, f"w1_g{a}0{pr}") for a in range(2) for pr in range(2)}
        w1_q = {}
        for pr in range(2):
            deal(nc.scalar.copy, w1_g[0, 0, pr], w1_raw[0, 0][0], pr, 0)
        for hf in range(2):
            nc.vector.tensor_copy(
                v_w[1][:, BANK * hf : BANK * (hf + 1)],
                tab_w[1][:].bitcast(U32).indirect(list1[:, 32 * hf : 32 * (hf + 1)]),
            )
            w1_q[0, 0, hf] = quantize(flat(w1_g[0, 0, hf]), f"w1_q00{hf}")
        for u in range(2):
            for pr in range(2):
                deal(nc.scalar.copy, w1_g[1, 0, pr], w1_raw[1, 0][u], pr, 64 * u)
        for pr in range(2):
            w1_q[1, 0, pr] = quantize(flat(w1_g[1, 0, pr]), f"w1_q10{pr}")

        def stage1_pass(acc, a, b, t, hf):
            codes, scales = w1_q[a, b, t // 2]
            wc = slice(P * (t % 2), P * (t % 2 + 1))
            sc = slice(BANK * hf, BANK * (hf + 1))
            nc.tensor.matmul_mx(
                out=acc[:],
                lhsT=codes[:, wc].bitcast(FP8X4),
                lhsT_scale=scales[:, wc],
                rhs=v_w[a][:, sc].bitcast(FP8X4),
                rhs_scale=v_s[4 * a : P, sc],
                start=(a == 0),
                stop=(a == 1),
            )

        h = {(b, t): tile([P, S], F32, f"h{b}{t}") for b in range(2) for t in range(PACK)}
        x = [tile([P, PACK, M], F32, f"x{b}") for b in range(2)]

        def evacuate(acc, b, t, hf):
            nc.scalar.activation(
                out=h[b, t][:, BANK * hf : BANK * (hf + 1)], in_=acc[:], func=ACT.Identity, bias=bias[:, b, t : t + 1]
            )

        def pick(b, t):
            nc.vector.tensor_tensor(x[b][:, t, :], h[b, t][:].indirect(list2[:]), wgt_sb[:], ALU.mult)

        accs = {(t, hf): bank() for t in range(PACK) for hf in range(2)}
        for a in range(2):
            for t in range(PACK):
                for hf in range(2):
                    stage1_pass(accs[t, hf], a, 0, t, hf)

        def first_block(t):
            for hf in range(2):
                if (t, hf) == (0, 1):
                    nc.vector.tensor_scalar(h[0, 0][:, BANK:], accs[t, hf][:], bias[:, 0, 0:1], None, ALU.add)
                else:
                    evacuate(accs[t, hf], 0, t, hf)
            pick(0, t)

        def second_block(t):
            for hf in range(2):
                acc = bank()
                for a in range(2):
                    stage1_pass(acc, a, 1, t, hf)
                evacuate(acc, 1, t, hf)
            pick(1, t)

        def deal_w1(a, pr):
            w1_g[a, 1, pr] = tile([P, 2, P, PACK], BF16, f"w1_g{a}1{pr}", tag=f"w1_q10{pr}_" + ("codes", "scales")[a])
            deal(nc.scalar.copy, w1_g[a, 1, pr], w1_raw[a, 1][0], pr, 0)
            w1_q[a, 1, pr] = quantize(flat(w1_g[a, 1, pr]), f"w1_q{a}1{pr}")

        lev_bf = tile([P, 2, 16, PACK], BF16, "lev_bf")
        x_bf = [tile([P, M, PACK], BF16, f"x_bf{b}") for b in range(2)]
        hi = [tile([P, M, PACK], BF16, f"hi{b}") for b in range(2)]
        lo = [tile([P, M, PACK], BF16, f"lo{b}") for b in range(2)]
        w2_g = {}
        w2_q, hi_q, lo_q = {}, {}, {}

        def weave(b, u):
            cols = slice(256 * u, 256 * (u + 1))
            nc.scalar.copy(
                out=x_bf[b][:, cols, :].rearrange("p (c i) t -> p c t i", i=4),
                in_=x[b][:, :, cols].rearrange("p t (c i) -> p c t i", i=4),
            )

        for b in range(2):
            lo_q[b] = (tile([P, M], U32, f"lo_codes{b}"), tile([P, M], U8, f"lo_scales{b}"))
            hi_q[b] = (tile([P, M], U32, f"hi_codes{b}"), tile([P, M], U8, f"hi_scales{b}"))

        def split(b, u):
            cols = slice(256 * u, 256 * (u + 1))
            lv = lev_bf[:, b : b + 1, :, :].rearrange("p b m t -> p b (m t)").to_broadcast([P, 16, 16 * PACK])
            for part, op in ((lo[b], ALU.min), (hi[b], ALU.max)):
                nc.vector.tensor_tensor(
                    part[:, cols, :].rearrange("p (c m) t -> p c (m t)", m=16),
                    x_bf[b][:, cols, :].rearrange("p (c m) t -> p c (m t)", m=16),
                    lv,
                    op,
                )
            for part, (codes, scales) in ((lo[b], lo_q[b]), (hi[b], hi_q[b])):
                nc.vector.quantize_mx(
                    out=codes[:, cols].bitcast(FP8X4),
                    scales=scales[:, cols],
                    in_=part[:, cols, :].rearrange("p m t -> p (m t)"),
                )

        def deal_w2(pr):
            for b in range(2):
                tag = ("w1_q111_" + ("codes", "scales")[b], f"x{b}")[pr]
                w2_g[b, pr] = tile([P, 2, P, PACK], BF16, f"w2_g{b}{pr}", tag=tag)
                deal(nc.scalar.copy, w2_g[b, pr], w2_raw[b], pr, 0)
                w2_q[b, pr] = quantize(flat(w2_g[b, pr]), f"w2_q{b}{pr}")

        first_block(0)
        first_block(1)
        deal_w1(0, 0)
        first_block(2)
        deal_w1(1, 0)
        w3_w = tile([P, 2, PACK, P, 2], U8, "w3_w", tag="w1_q100_scales")
        nc.vector.tensor_copy(
            out=w3_w[:].rearrange("p a t q e -> p a t (q e)").bitcast(U16),
            in_=w3_w_raw[:].bitcast(U16).rearrange("p a (q t) -> p a t q", t=PACK),
        )
        first_block(3)
        second_block(0)
        deal_w1(0, 1)
        w3_s = tile([P, 2, PACK, P], U8, "w3_s", tag="w1_q101_codes")
        nc.vector.tensor_copy(out=w3_s[:], in_=w3_s_raw[:].rearrange("p a (q t) -> p a t q", t=PACK))
        second_block(1)
        deal_w1(1, 1)
        nc.scalar.copy(out=lev_bf[:], in_=lev[:, :, 0:PACK].unsqueeze(2).to_broadcast([P, 2, 16, PACK]))
        weave(0, 0)
        split(0, 0)
        second_block(2)
        second_block(3)
        weave(0, 1)
        split(0, 1)
        for u in range(2):
            weave(1, u)
            split(1, u)
        deal_w2(0)
        deal_w2(1)

        y1 = [bank() for t in range(PACK)]
        y2 = [bank() for t in range(PACK)]

        def y2_pass(b, t):
            codes, scales = lo_q[b]
            nc.tensor.matmul_mx(
                out=y2[t][:],
                lhsT=w3_w[:, b, t, :, :].rearrange("p q e -> p (q e)").bitcast(FP4X4),
                lhsT_scale=w3_s[:, b, t, :],
                rhs=codes[:].bitcast(FP8X4),
                rhs_scale=scales[:],
                start=(b == 0),
                stop=(b == 1),
            )

        def y1_pass(b, t):
            codes, scales = hi_q[b]
            w_codes, w_scales = w2_q[b, t // 2]
            wc = slice(P * (t % 2), P * (t % 2 + 1))
            nc.tensor.matmul_mx(
                out=y1[t][:],
                lhsT=w_codes[:, wc].bitcast(FP8X4),
                lhsT_scale=w_scales[:, wc],
                rhs=codes[:].bitcast(FP8X4),
                rhs_scale=scales[:],
                start=(b == 0),
                stop=(b == 1),
            )

        for b in range(2):
            for t in range(PACK):
                y2_pass(b, t)
            for t in range(PACK):
                y1_pass(b, t)

        out_rows = out.rearrange("(p t) c -> p t c", t=PACK)
        first = [tile([P, M], F32, f"first{t}", tag=f"w1_g{t // 2}0{t % 2}") for t in range(PACK)]
        second = [tile([P, M], F32, f"second{t}") for t in range(PACK)]

        def factors(t):
            nc.vector.scalar_tensor_tensor(second[t][:], y2[t][:], 1.0, wgo_sb[:], ALU.add, ALU.mult)
            nc.scalar.copy(out=first[t][:], in_=y1[t][:])

        factors(0)
        for t in range(PACK):
            if t + 1 < PACK:
                factors(t + 1)
            nc.vector.tensor_tensor(pages[t][:].indirect(list3[:]), first[t][:], second[t][:], ALU.mult)
            nc.sync.dma_start(out=out_rows[:, t, :], in_=pages[t][:])
